import numpy as np, ml_dtypes
CORES = [9,25,41,57]
N = 4
BF = ml_dtypes.bfloat16
def gentries(a):
    return np.ascontiguousarray(a.reshape(8, 16, -1).transpose(0, 2, 1)).reshape(8, -1)
def gtable(e):
    e = np.asarray(e); return np.ascontiguousarray(e.reshape(8, -1, 16).transpose(0, 2, 1)).reshape(128, -1).astype(np.int32)
W, K, E, X, S, RO = 8192, 1536, 128, 4, 3, 3
ANY = np.arange(256); LEN = np.arange(1, 13)
def place(u1, u2, m):
    return ((((u1 & 4095) * (u2 & 4095)) >> 5) + u2 + 97 * m) & (W - 1)
def hashes(st, m, wt):
    u = np.where(np.arange(12) < m[:, None], st, 0) @ wt
    return place(u[:, 0], u[:, 1], m)
def ropes(rng, shape, lens):
    n = np.minimum(rng.integers(0, 8, shape), 4)
    return np.where(np.arange(4) < n[..., None], lens[rng.integers(0, len(lens), shape + (4,))], 0)
def fill(rng):
    return np.concatenate([rng.integers(0, 256, (N, 8, 12, W)), np.moveaxis(ropes(rng, (N, 8, W), LEN), 3, 2)], axis=2)
def pool(rng, M, vals):
    st = vals[rng.integers(0, len(vals), (M, 12))]; h = max(M // 8, 1); keep = rng.integers(0, 13, M); keep[:h] = 0
    return np.where(np.arange(12) < keep[:, None], st[rng.integers(0, h, M)], st)
def plant(T, st, m, ro, wt):
    h = hashes(st, m, wt); T[:, h] = np.concatenate([st.T, ro.T])
def asks(rng, st, vals, lens):
    x = st[rng.integers(0, len(st), K)]; cut = np.where(rng.random(K) < 0.3, rng.integers(0, 13, K), 12)
    x = np.where(np.arange(12) < cut[:, None], x, vals[rng.integers(0, len(vals), (K, 12))])
    return np.concatenate([x.T, ropes(rng, (K,), lens).T])
def parts(rng, wt, M, n, vals, lens):
    P = fill(rng); q = np.zeros((N, 8, 16, K), np.int64)
    for g in range(8):
        st = pool(rng, int(M[g]), vals)
        for a in range(N):
            plant(P[a, g], st[rng.integers(0, len(st), n)], lens[rng.integers(0, len(lens), n)], ropes(rng, (n,), lens), wt[a, g])
            q[a, g] = asks(rng, st, vals, lens)
    return P, q
def alike_ropes(n, l):
    return np.tile(np.array((tuple(l) + (0, 0, 0, 0))[:4]), (n, 1))
def steer(rng, c):
    v = ((np.diff(c, axis=1, prepend=0) - 194) & (W - 1)) + W * rng.integers(0, 65280 // W, c.shape)
    return np.stack([v % 255, v // 255], axis=2).reshape(len(c), 12)
def meetings(rng, ends):
    n = 6; F = 2 + 2 * S; cut = 2 + n * np.arange(7); four = (6, 8, 10, 12)
    c = 1 + rng.permutation(W - 2)[:(2 + 7 * n) * 6].reshape(-1, 6)
    d, s1, e1, q2, s3, o3, q4, s5 = np.split(c, cut)
    for i in range(2): d[i, ends[i][0]] = ends[i][1]
    s1[:, 1] = s1[:, 0]; e1[:, 0] = s1[:, 0]
    q2[:, S] = q2[:, 1]
    s3[:, S - 1] = s3[:, S]; o3[:, :2] = s3[:, :2]
    q4[:, 3] = q4[:, 1]
    s5[:, 5] = s5[:, 2]
    x = steer(rng, c); d, s1, e1, q2, s3, o3, q4, s5 = np.split(x, cut)
    e1[:, :2] = s1[:, :2]; o3[:, :4] = s3[:, :4]
    r2 = q2.copy(); r2[:, 4:] = (r2[:, 4:] + rng.integers(1, 256, (n, 8))) & 255
    r4 = q4.copy(); r4[:, 4:] = (r4[:, 4:] + rng.integers(1, 256, (n, 8))) & 255
    marks = [(d, 4, four), (d, F + 2, ()), (s1, 4, four), (s1, F + 2, ()), (r2, 4, four), (q2, F + 2, ()), (s3, 4, four), (s3, F + 2, ()), (o3, F, ()), (r4, 4, ()), (s5, 4, (6,))]
    ask = [(d, (4,)), (s1, (4,)), (q2, (F,)), (s3, (4,)), (o3, (4,)), (q4, (8,)), (s5, (4,)), (s5, (12,)), (e1, (12, 2)), (q2, (4,)), (q4, (8, 4))]
    return marks, np.concatenate([y for y, l in ask]), np.concatenate([alike_ropes(len(y), l) for y, l in ask]), 2 + 7 * n
def pack(P, q, wt):
    w = np.concatenate([wt, np.zeros((N, 8, 4, 2), np.int64)], axis=2)
    return {"mk": P.reshape(N, 128, W).astype(np.float32).astype(BF), "qs": q.reshape(N, 128, K).astype(np.float32).astype(BF), "wt": w.reshape(N, 128, 2).astype(np.float32).astype(BF)}
def setup_inputs(rng):
    wt = rng.integers(0, 256, (N, 8, 12, 2)); P, q = parts(rng, wt, [512] * 8, 3 * W // 4, ANY, LEN)
    return pack(P, q, wt)
def setup_inputs_alike(rng):
    wt = rng.integers(0, 256, (N, 8, 12, 2)); P, q = parts(rng, wt, rng.integers(16, 33, 8), 160, ANY, LEN)
    return pack(P, q, wt)
def setup_inputs_ends(rng):
    wt = rng.choice(np.array([0, 1, 255]), (N, 8, 12, 2)); wt[:, 3] = 0; wt[:, 5] = 255
    for g in (0, 1, 6):
        wt[:, g] = 0; wt[:, g, 0::2, 1] = 1; wt[:, g, 1::2, 1] = 255
    P, q = parts(rng, wt, [64] * 8, W // 4, np.array([0, 255, 0, 1, 254]), np.array([1, 12, 1, 12, 2, 11]))
    for g, ends in ((0, ((S, 0), (1, W - 1))), (1, ((S + 1, 0), (S + 1, W - 1))), (6, ((S, W - 1), (1, 0)))):
        marks, st, ro, look = meetings(rng, ends)
        for a in range(N):
            for y, m, l in marks: plant(P[a, g], y, np.full(len(y), m), alike_ropes(len(y), l), wt[a, g])
            j = np.concatenate([rng.permutation(len(st)), rng.integers(0, look, K - len(st))])
            q[a, g] = np.concatenate([st[j].T, ro[j].T])
    x = rng.integers(225, 256, (2048, 12)); x = x[np.unique(np.sum(x, axis=1), return_index=True)[1]]
    u = 255 * np.sum(x, axis=1); x = x[np.argsort(-((((u & 4095) ** 2) >> 5) + u))[:24]]
    for a in range(N):
        plant(P[a, 5], x, np.full(len(x), 12), np.zeros((len(x), 4), np.int64), wt[a, 5])
        t = rng.permutation(K)[:96]; q[a, 5][:12, t] = x[np.arange(96) % len(x)].T; q[a, 5][12:, t] = np.array([12, 0, 0, 0])[:, None]
    return pack(P, q, wt)
def setup_inputs_full(rng):
    w = rng.integers(0, 256, (8, 12, 2)); wt = np.stack([w] * N); P = fill(rng); q = np.zeros((N, 8, 16, K), np.int64)
    for g in range(8):
        st = rng.integers(0, 256, (2048, 12)); hs = np.stack([hashes(st, np.full(2048, m), w[g]) for m in [5] + [9 + i for i in range(S)]])
        used = set(); keep = []
        for i in range(2048):
            c = set(hs[:, i].tolist())
            if len(keep) < E and len(c) == S + 1 and not (c & used):
                used |= c; keep.append(i)
        x = st[np.array(keep)]; n = len(keep)
        for a in range(N):
            plant(P[a, g], x, np.full(n, 5), np.stack([np.array([9, 10, 11, 12])] * n), w[g])
            plant(P[a, g], x, np.full(n, 8 + S), np.zeros((n, 4), np.int64), w[g])
            j = np.concatenate([rng.permutation(n), rng.integers(0, n, K - n)])
            first = (rng.random(K) < 0.5) | (np.arange(K) < n)
            ro = np.where(first[:, None], np.array([5, 8, 0, 0]), np.array([7 + S, 5, 12, 0]))
            q[a, g] = np.concatenate([x[j].T, ro.T])
    return pack(P, q, wt)
def setup_inputs_still(rng):
    wt = rng.integers(0, 256, (N, 8, 12, 2)); P, q = parts(rng, wt, [256] * 8, W // 2, ANY, LEN); e = rng.permutation(8)
    q[:, :, 12:] = np.where(rng.random((N, 8, 1, K)) < 0.5, 0, q[:, :, 12:])
    q[:, e[0], 12:] = 0; P[:, e[1], 12:] = 0; q[:, e[2], :12] = rng.integers(0, 256, (N, 12, K))
    q[:, e[2], 12:] = np.where(q[:, e[2], 12:] > 0, np.maximum(q[:, e[2], 12:], 4), 0)
    return pack(P, q, wt)
def setup_inputs_spread(rng):
    vals = np.minimum(np.exp2(8.01 * rng.random(512)).astype(np.int64), 256) - 1
    wt = vals[rng.integers(0, 512, (N, 8, 12, 2))]; P, q = parts(rng, wt, 2 ** rng.integers(3, 12, 8), W // 2, vals, LEN)
    return pack(P, q, wt)
def check_inputs(d):
    bad = []
    for k, n in (("mk", W), ("qs", K), ("wt", 2)):
        v = np.asarray(d[k]).astype(np.float32).reshape(N, 8, 16, n)
        if not np.all(v == np.floor(v)): bad.append("whole numbers of " + k)
        if not (np.min(v) >= 0 and np.max(v[:, :, :12]) <= 255): bad.append("range of " + k)
        if not np.max(v[:, :, 12:]) <= (0 if k == "wt" else 12): bad.append("last four rows of " + k)
        if k != "wt" and np.any((v[:, :, 12:15] == 0) & (v[:, :, 13:] > 0)): bad.append("ropes of " + k)
    return bad
def reference(mk, qs, wt):
    P = mk.astype(np.float32).astype(np.int32).reshape(N, 8, 16, W); q = qs.astype(np.float32).astype(np.int32).reshape(N, 8, 16, K)
    w = np.ascontiguousarray(wt.astype(np.float32).astype(np.int32).reshape(N, 8, 16, 2)[:, :, :12].transpose(0, 1, 3, 2))
    p = np.arange(12, dtype=np.int32)[:, None]
    for rnd in range(RO):
        sy = q[:, :, :12]; ro = q[:, :, 12:]
        b = np.full((N, 8, K), -1, np.int32); f = np.full((N, 8, K), -1, np.int32); mb = np.zeros((N, 8, K), np.int32); mf = np.zeros((N, 8, K), np.int32)
        for step in range(S):
            m = ro[:, :, 0]
            u = np.matmul(w, np.where(p < m[:, :, None], sy, 0))
            h = place(u[:, :, 0], u[:, :, 1], m)
            v = np.take_along_axis(P, h[:, :, None], axis=3)
            same = np.all((v[:, :, :12] == sy) | (p >= m[:, :, None]), axis=2)
            hit = (m > 0) & same; miss = (m > 0) & ~same
            b = np.where(hit, h, b); mb = np.where(hit, m, mb)
            f = np.where(miss, h, np.where(hit, -1, f)); mf = np.where(miss, m, mf)
            less = np.concatenate([ro[:, :, 1:], np.zeros((N, 8, 1, K), np.int32)], axis=2)
            ro = np.where(hit[:, :, None], v[:, :, 12:], np.where(miss[:, :, None], less, ro))
        old = np.take_along_axis(P, np.maximum(b, 0)[:, :, None], axis=3)[:, :, :12]
        new = q.copy(); new[:, :, :12] = np.where((b >= 0)[:, :, None] & (p < mb[:, :, None] + X), old, sy)
        if rnd < RO - 1:
            for a in range(N):
                for g in range(8):
                    T = P[a, g]; c = np.nonzero((b[a, g, :E] >= 0) & (f[a, g, :E] >= 0))[0]
                    t = c[np.unique(f[a, g, c], return_index=True)[1]]
                    T[:, f[a, g, t]] = np.concatenate([sy[a, g][:, t], ro[a, g][:, t]])
                    t = c[np.unique(b[a, g, c], return_index=True)[1]]
                    have = T[12:15, b[a, g, t]]
                    T[12:, b[a, g, t]] = np.concatenate([mf[a, g, t][None], have])
            q = np.ascontiguousarray(new.reshape(N, 8, 16, N, K // N).transpose(3, 1, 2, 0, 4)).reshape(N, 8, 16, K)
    return {"yq": new.reshape(N, 128, K).astype(np.float32).astype(BF), "yb": np.stack([gtable(x) for x in b]).astype(np.float32)}

from concourse.mybir import AluOpType, AxisListType, ActivationFunctionType

OP = AluOpType
AF = ActivationFunctionType
W, K, NB = 8192, 1536, 384
WT = W + 128
NJ, CH = 48, 768
TP = 112
DS = 192
MAGIC = 1.5 * 2.0 ** 36

_F, _B, _I, _U = "float32", "bfloat16", "int32", "uint16"
_BUFS = {"mks": (W + 256, _B), "kt": (WT, _F), "wtb": (2, _B), "wtf": (2, _F), "pint": (8, _I), "dif": (128, _F),
         "tidx": (256, _F), "cc": (32, _F), "gs": (8, _F), "rw": (32, _B), "rd": (24, _B), "rp": (48, _B),
         "re0": (288, _B), "re1": (288, _B), "rc": (288, _B), "rcf": (96, _F), "yb_s": (96, _F),
         "efi": (8, _I), "efc": (8, _I), "emf": (8, _I), "ekk": (8, _I), "eof": (16, _U), "eok": (8, _U), "eom": (8, _U),
         "eow": (16, _U), "eka": (256, _F), "ey": (2048, _F), "ifp": (128, _F)}
for _n in ("q0", "q1", "q2", "n0", "n1", "n2"):
    _BUFS[_n] = (K, _B)
for _n in ("col", "trb", "tr", "half", "eh", "c10", "zer", "thr", "pw", "ep", "m1", "m2", "m3", "m4", "m5", "emg", "ecf", "eyf", "ef",
           "eg", "eed", "eu", "ev", "efb", "en1", "enb", "emn", "els", "eg2", "eg3", "efn"):
    _BUFS[_n] = (16, _F)
for _n in ("mt", "ml", "k1"):
    _BUFS[_n] = (16, _B)
for _n in ("ib", "inb", "i32b", "sym", "sh1", "sh2", "sh12", "sd1", "sd", "sel", "evv", "ev1", "eww", "emm", "ezz", "enn"):
    _BUFS[_n] = (128, _B)
_CB = {"z": (CH, _B), "d": (CH, _B), "ui": (128, _I), "ua": (128, _I), "up": (64, _I), "uk": (64, _I), "us": (144, _F),
       "uq": (144, _B), "off": (NJ, _U), "mo": (NJ, _U), "moA": (NJ, _U), "moB": (NJ, _U), "ms": (NJ, _B), "msA": (NJ, _B),
       "msB": (NJ, _B), "cod": (NJ, _F), "an": (64, _F), "hit": (144, _B), "x0": (144, _B), "x1": (144, _B), "x2": (144, _B),
       "e1": (64, _F), "sv": (256, _B), "y": (NJ, _F), "bb": (NJ, _F), "bi": (NJ, _I), "bm": (NJ, _I), "bc": (NJ, _I),
       "ofb": (NJ, _U), "ofm": (NJ, _U), "nb": (NJ, _F), "rtA": (432, _B), "rtB": (432, _B), "zcA": (192, _F), "zcB": (192, _F),
       "dl": (CH, _B), "zl": (CH, _B)}
for _c in range(2):
    for _n in _CB:
        _BUFS["%s_%d" % (_n, _c)] = _CB[_n]
SCRATCH, PLACE = {}, {}
for _n in _BUFS:
    _w, _t = _BUFS[_n]
    if _w <= 512 and _n not in ("wtb", "re0", "re1", "yb_s"):
        _p = "pack_" + _t
        _o = SCRATCH[_p][1][1] if _p in SCRATCH else 0
        SCRATCH[_p] = ("sbuf", [128, _o + (_w + 15) // 16 * 16], _t)
        PLACE[_n] = (_p, _o)
    else:
        SCRATCH[_n] = ("sbuf", [128, _w], _t)
        PLACE[_n] = (_n, 0)
for _n in ("psU_0", "psU_1", "psD_0", "psD_1", "psE_0", "psE_1", "psL0", "psL1"):
    SCRATCH[_n] = ("psum", [128, 512], _F)
    PLACE[_n] = (_n, 0)
SEMAPHORES = ["sV", "sS", "sP", "sG", "loc"] + ["d%d" % i for i in range(16)] + ["ax%d" % i for i in range(4)] \
    + ["a%d_%d" % (r, i) for r in (1, 2) for i in range(4)]


def rank_program(g, core, T, topo):
    rank = T.rank_of(core)
    if rank is None:
        return
    ops = []
    hist = {}
    ndma = [0]
    CY = 0.00083 * 1.2
    LAT = 0.06

    def A(b, lo, hi, st=1, p=128, base=0):
        n, k = PLACE[b]
        t = T[n]
        return (t[base:base + p, k + lo:k + hi] if st == 1 else t[base:base + p, k + lo:k + hi:st], [(b, lo, hi)], [])

    def IND(b, lo, hi, o, a, z):
        (n, k), (m, i) = PLACE[b], PLACE[o]
        return (T[n][:, k + lo:k + hi].indirect(T[m][:, i + a:i + z]), [(b, lo, hi)], [(o, a, z)])

    def add(eng, fn, outs, ins, cost, cnt=1, sem=None, val=None, extra=(), lat=0.0):
        rd, wr = [], []
        for x in ins:
            rd += x[1] + x[2]
        for x in outs:
            wr += x[1]
            rd += x[2]
        o = {"i": len(ops), "eng": eng, "fn": fn, "cost": cost, "cnt": cnt, "sem": sem, "val": val, "dep": {}, "lat": lat}
        for k, acc in (("r", rd), ("w", wr)):
            for b, lo, hi in acc:
                for p, pk, pl, ph in hist.get(b, ()):
                    if pl < hi and lo < ph and (k == "w" or pk == "w"):
                        o["dep"][p["i"]] = 1
                    elif b[:2] == "ps" and p["eng"] != eng:
                        o["dep"][p["i"]] = 1
        for e in extra:
            o["dep"].setdefault(e["i"], 0)
        o["dep"].pop(o["i"], None)
        for k, acc in (("r", rd), ("w", wr)):
            for b, lo, hi in acc:
                h = hist.setdefault(b, [])
                if k == "w" and b[:2] != "ps":
                    h[:] = [x for x in h if not (lo <= x[2] and x[3] <= hi)]
                h.append((o, k, lo, hi))
        ops.append(o)
        return o

    def vc(n, two=False):
        return max(64, n * (2 if two else 1)) * CY + 0.02

    def gc(n):
        return 0.05 + n * 1.56 * CY

    def v_tt(out, a, b, op, n, ind=False, two=False):
        return add("V", lambda inc: inc(g.vector.tensor_tensor(out[0], a[0], b[0], op)), [out], [a, b], gc(n) if ind else vc(n, two))

    def v_ts(out, a, s1, s2, op0, op1, n):
        ins = [a] + [s for s in (s1, s2) if isinstance(s, tuple)]
        x1 = s1[0] if isinstance(s1, tuple) else s1
        x2 = s2[0] if isinstance(s2, tuple) else s2
        if op1 is None:
            f = lambda inc: inc(g.vector.tensor_scalar(out[0], a[0], x1, None, op0))
        else:
            f = lambda inc: inc(g.vector.tensor_scalar(out[0], a[0], x1, x2, op0, op1))
        return add("V", f, [out], ins, vc(n))

    def v_cp(out, a, n, cost=None):
        return add("V", lambda inc: inc(g.vector.tensor_copy(out[0], a[0])), [out], [a], cost or vc(n))

    def v_ms(out, c, n):
        return add("V", lambda inc: inc(g.vector.memset(out[0], c)), [out], [], vc(n))

    def s_act(out, a, n, func=None, bias=None, scale=1.0, ind=False):
        f = func or AF.Identity
        ins = [a] + ([bias] if isinstance(bias, tuple) else [])
        if bias is None:
            fn = lambda inc: inc(g.scalar.activation(out[0], a[0], f, scale=scale))
        else:
            b = bias[0] if isinstance(bias, tuple) else bias
            fn = lambda inc: inc(g.scalar.activation(out[0], a[0], f, bias=b, scale=scale))
        return add("S", fn, [out], ins, gc(n) + 0.02 if ind else max(64, n) * CY + 0.04)

    def pe(mms, cost):
        def fn(inc):
            for o, l, r, a, z in mms:
                inc(g.tensor.matmul(o[0], l[0], r[0], a, z))
        return add("P", fn, [m[0] for m in mms], [m[1] for m in mms] + [m[2] for m in mms], cost * CY + 0.03, cnt=len(mms))

    def g_iota(out, pattern, base, mul, n, flag):
        if flag:
            f = lambda inc: inc(g.iota(out[0], pattern, base, mul, allow_small_or_imprecise_dtypes=True))
        else:
            f = lambda inc: inc(g.iota(out[0], pattern, base, mul))
        return add("G", f, [out], [], 0.13 + 2 * n * CY)

    def dma(eng, out, a, cost):
        s = "d%d" % ndma[0]
        ndma[0] += 1
        q = g.sync if eng == "Q" else g.scalar
        return add(eng, lambda inc: q.dma_start(out[0], a[0]).then_inc(T.sem[s], 16), [out], [a], 0.1, sem=s, val=16, lat=cost)

    nsend = [0]

    def send(dst, out_ap, a, rsem):
        rid, pid, _se = topo.addr(dst)
        mask = topo.mask(core, dst)
        nsend[0] += len(topo.engines(core, dst))
        return add("G", lambda inc: g.remote_dma(out_ap=out_ap, in_ap=a[0], remote_sem=T.sem[rsem], local_sem=T.sem["loc"], pid=pid,
                                                 routing_id=rid, dma_engine_mask=mask), [], [a], 1.0, sem="", val=0)

    arrivals = []
    CO = (0, 1) if rank < 2 else (1, 0)

    def arrive(out, src, rsem, after, cost):
        v = len(topo.engines(T.cores[src], core))
        arrivals.append((rsem, v))
        return add("X", None, [out], [], 0.0, sem=rsem, val=v, extra=after, lat=cost)

    others = [s for s in range(len(T.cores)) if s != rank]

    ext = lambda x: (x, [], [])
    dma("Q", A("q0", 0, K), ext(T.qs[:]), 3.5)
    dma("S", A("wtb", 0, 2), ext(T.wt[:]), 2.5)
    dma("Q", A("mks", 0, W // 2), ext(T.mk[:, 0:W // 2]), 6.0)
    dma("S", A("mks", W // 2, W), ext(T.mk[:, W // 2:W]), 6.0)
    g_iota(A("pint", 0, 1), [[0, 1]], 0, 1, 1, False)
    g_iota(A("col", 0, 16), [[1, 16]], 0, 0, 16, True)
    g_iota(A("dif", 0, 128), [[1, 128]], 0, -1, 128, True)
    v_ts(A("pint", 1, 2), A("pint", 0, 1), 15, None, OP.bitwise_and, None, 1)
    v_ts(A("pint", 2, 3), A("pint", 0, 1), 4, None, OP.arith_shift_right, None, 1)
    IP, GP, IP4, LT, G12, G13, M1213, NE12, E1415, WN, DA, DB, DC, W3A, W3B, W3, M1214 = [A("cc", i, i + 1) for i in range(17)]
    E = lambda k: A("eh", k, k + 1)
    v_cp(IP, A("pint", 1, 2), 1)
    v_cp(GP, A("pint", 2, 3), 1)
    COL = A("col", 0, 16)
    v_ts(A("eh", 0, 16), COL, IP, None, OP.is_equal, None, 16)
    v_ts(A("gs", 0, 8), A("col", 0, 8), GP, None, OP.is_equal, None, 8)
    GS = A("gs", 0, 8)
    v_tt(DA, E(12), E(14), OP.subtract, 1)
    v_tt(DB, E(12), E(13), OP.subtract, 1)
    v_tt(DC, E(13), E(14), OP.subtract, 1)
    for i, c in enumerate((E(12), E(13), E(14), DB, DC, DA)):
        v_ts(A("rp", 8 * i, 8 * i + 8), GS, c, None, OP.mult, None, 8)
    DIF = A("dif", 0, 128)
    v_ts(A("ib", 0, 128), DIF, 0.0, None, OP.is_equal, None, 128)
    v_ms(A("c10", 0, 16), 2.0 ** -10, 16)
    v_ms(A("zer", 0, 16), 0.0, 16)

    def scan(b, lo, hi, ini):
        o, x, y = A(b, lo, hi), A("c10", lo, hi), A("zer", lo, hi)
        add("V", lambda inc: inc(g.vector.tensor_tensor_scan(o[0], x[0], y[0], ini, OP.mult, OP.add)), [o], [x, y], vc(16))

    v_ms(A("thr", 0, 1), 0.0, 1)
    scan("thr", 1, 16, -2.0 ** 59)
    v_ts(LT, IP, 12.0, None, OP.is_lt, None, 1)
    v_tt(E1415, E(14), E(15), OP.add, 1)
    M = [A("m%d" % i, 0, 16) for i in range(1, 6)]
    v_ts(M[0], COL, IP, 256.0, OP.is_gt, OP.mult, 16)
    v_ts(M[1], M[0], LT, None, OP.mult, None, 16)
    v_ts(M[2], COL, E(12), -1.0, OP.mult, OP.mult, 16)
    v_ts(M[3], A("thr", 0, 16), E(13), None, OP.mult, None, 16)
    v_tt(M[0], M[1], M[2], OP.add, 16)
    v_tt(M[4], M[0], M[3], OP.add, 16)
    v_ts(A("mt", 0, 16), M[4], E1415, None, OP.subtract, None, 16)
    v_cp(A("wtf", 0, 2), A("wtb", 0, 2), 2)
    v_ts(W3A, E(12), -97.0, A("wtf", 1, 2), OP.mult, OP.add, 1)
    v_ts(W3B, E(14), 4096.0, W3A, OP.mult, OP.add, 1)
    v_ts(W3, E(15), -0.5, W3B, OP.mult, OP.add, 1)
    v_ts(A("rw", 0, 8), GS, A("wtf", 0, 1), None, OP.mult, None, 8)
    v_ts(A("rw", 8, 16), GS, A("wtf", 1, 2), None, OP.mult, None, 8)
    v_ts(A("rw", 16, 24), GS, W3, None, OP.mult, None, 8)
    v_ts(A("rw", 24, 32), GS, E(13), -1.0, OP.mult, OP.mult, 8)
    v_ts(A("ifp", 0, 128), DIF, 0.0, None, OP.is_equal, None, 128)
    v_ts(A("inb", 0, 128), DIF, 0.0, -1.0, OP.is_equal, OP.mult, 128)
    v_ts(A("i32b", 0, 128), DIF, 0.0, 1.0 / 32, OP.is_equal, OP.mult, 128)
    scan("pw", 0, 12, 2.0 ** 60)
    v_ms(A("pw", 12, 16), 0.0, 4)
    v_tt(A("ep", 0, 16), A("eh", 0, 16), A("pw", 0, 16), OP.mult, 16)
    epx = A("ep", 0, 16)
    add("V", lambda inc: inc(g.vector.tensor_reduce(WN[0], epx[0], AxisListType.X, OP.add)), [WN], [epx], vc(16))
    for i, c in enumerate((WN, E(12), E(13))):
        v_ts(A("rd", 8 * i, 8 * i + 8), GS, c, None, OP.mult, None, 8)
    for c in CO:
        v_ms(A("psL%d" % c, 0, 384, p=64), 0.0, 384)
        v_ms(A("psU_%d" % c, 0, 256, p=64), 0.0, 256)
        v_ms(A("psD_%d" % c, 0, 192, p=64), 0.0, 192)
        for x in "AB":
            v_ms(A("rt%s_%d" % (x, c), 0, 432), 0.0, 216)
        for b in ("us", "uq", "hit", "x0", "x1", "x2"):
            v_ms(A("%s_%d" % (b, c), 0, 144), 0.0, 144 if b == "us" else 72)
    v_ms(A("mks", W, W + 256), 0.0, 128)

    def TL(b, src, off, rhs, nq):
        return [(A(b, j, 64 * nq, 8, NJ, 64 * h), A(src, off + 2 * j + h, off + CH, 16), rhs, True, True) for j in range(8) for h in range(2)]

    def LL(b, lo, terms):
        o = A(b, lo, lo + NJ)
        m = [(o, A(v, k + 1 - h, k + 129 - h, p=TP), A(i, 64 * h, 64 * h + NJ, p=TP)) for v, k, i in terms for h in range(2)]
        return [x + (i == 0, i == len(m) - 1) for i, x in enumerate(m)]

    def keep_ropes(x, c):
        b = "psL%d" % c
        for k in range(3):
            s_act(A("rt%s_%d" % (x, c), 144 * k + 1, 144 * k + 129, 2, TP), A(b, 64 * k, 64 * k + 64, p=TP), 64)
        s_act(A("zc%s_%d" % (x, c), 0, 192, p=TP), A(b, 192, 384, p=TP), 192)

    for c in CO:
        pe(TL("psL%d" % c, "q0", c * CH, A("rp", 0, 48), 6), 16 * 48)
        keep_ropes("A", c)
        e = "psE_%d" % c
        pe([m for k in range(3) for m in LL(e, NJ * k, [("rtA_%d" % c, 144 * k, "ib")])], 6 * 64)
        v_cp(A("moA_%d" % c, 0, NJ), A(e, 0, NJ), NJ)
        s_act(A("msA_%d" % c, 0, NJ), A(e, 0, NJ), NJ)
        for h in range(2):
            for k in range(3):
                o = (2 * c + h) * 72 + 24 * k
                s_act(A("re0", o, o + 24), A(e, NJ * k + 24 * h, NJ * k + 24 * h + 24), 24)
    sent = [send(T.cores[s], T["re1"][:, 72 * rank:72 * rank + 72], A("re0", 72 * s, 72 * s + 72), "ax%d" % rank) for s in others]
    for s in others:
        arrive(A("re1", 72 * s, 72 * s + 72), s, "ax%d" % s, sent, 4.0)
    g_iota(A("tidx", 0, 256), [[0, 2], [1, 128]], 0, 0, 256, True)
    g_iota(A("trb", 0, 16), [[0, 2], [16, 8]], W, 0, 16, True)
    g_iota(A("kt", 0, WT), [[128, WT]], 0, 0, WT, True)

    def late_constants():
        v_ts(IP4, IP, -4.0, None, OP.add, None, 1)
        v_ts(A("ml", 0, 16), COL, IP4, LT, OP.is_gt, OP.mult, 16)
        v_ms(A("ml", 0, 1), 0.0, 1)
        v_ts(A("k1", 0, 16), COL, 2.0, None, OP.is_equal, None, 16)
        v_ts(A("tr", 0, 16), A("trb", 0, 16), IP, None, OP.add, None, 16)
        v_ts(A("half", 0, 16), A("tr", 0, 16), -8193.0, 0.5, OP.add, OP.mult, 16)
        v_ts(G12, IP, 12.0, None, OP.is_gt, None, 1)
        v_ts(G13, IP, 13.0, None, OP.is_gt, None, 1)
        v_tt(M1213, E(12), E(13), OP.add, 1)
        v_tt(M1214, M1213, E(14), OP.add, 1)
        v_ts(NE12, E(12), -1.0, None, OP.mult, None, 1)
        v_ts(A("sym", 0, 128), DIF, 0.0, LT, OP.is_equal, OP.mult, 128)
        v_ts(A("sh1", 0, 128), DIF, -1.0, G12, OP.is_equal, OP.mult, 128)
        v_ts(A("sh2", 0, 128), DIF, -2.0, G13, OP.is_equal, OP.mult, 128)
        v_tt(A("sh12", 0, 128), A("sh1", 0, 128), A("sh2", 0, 128), OP.subtract, 128, two=True)
        v_ts(A("sd1", 0, 128), DIF, 1.0, M1214, OP.is_equal, OP.mult, 128)
        v_tt(A("sd", 0, 128), A("sd1", 0, 128), A("sym", 0, 128), OP.add, 128, two=True)
        v_ts(A("sel", 0, 128), DIF, 0.0, NE12, OP.is_equal, OP.mult, 128)

    def ropes_b():
        for s in range(len(T.cores)):
            for k in range(3):
                f = A("re0" if s == rank else "re1", 72 * s + 24 * k, 72 * s + 24 * k + 24)
                s_act(A("rc", 96 * k + 24 * s, 96 * k + 24 * s + 24), f, 24)
                if k == 0:
                    s_act(A("rcf", 24 * s, 24 * s + 24), f, 24)
        for c in CO:
            m = []
            for h in range(2):
                for k, ab in enumerate(((0,), (1,), (2,), (0, 1), (1, 2), (0, 2))):
                    o = A("psL%d" % c, 64 * k, 64 * k + 64, 1, NJ, 64 * h)
                    for i, n in enumerate(ab):
                        m.append((o, A("rc", 96 * n + NJ * c, 96 * n + NJ * c + NJ), A("inb" if i else "ib", h, 128, 2), i == 0, i == len(ab) - 1))
            pe(m, len(m) * 64)
            keep_ropes("B", c)
            s_act(A("msB_%d" % c, 0, NJ), A("rc", NJ * c, NJ * c + NJ), NJ)
            v_cp(A("moB_%d" % c, 0, NJ), A("rcf", NJ * c, NJ * c + NJ), NJ)

    def step(r, s, c):
        x = "AB"[r % 2]
        n = lambda b: "%s_%d" % (b, c)
        P = lambda b_, lo, hi: A(n(b_), lo, hi, p=TP)
        PD = lambda b_: A(n(b_), 1, 129, 2, TP)
        qb, b = "q%d" % r, c * CH
        mo, mf = (n("mo" + x), n("ms" + x)) if s == 0 else (n("mo"), n("ms"))
        U, D, Ep = n("psU"), n("psD"), n("psE")
        v_tt(A(n("z"), 0, CH), IND("mt", 0, 16, mo, 0, NJ), A(qb, b, b + CH), OP.min, CH, ind=True)
        pe(TL(U, n("z"), 0, A("rw", 0, 32), 4), 16 * 48)
        v_cp(P("ui", 0, 128), P("psU", 0, 128), 128)
        v_ts(P("ua", 0, 128), P("ui", 0, 128), 4095, None, OP.bitwise_and, None, 128)
        v_tt(P("up", 0, 64), P("ua", 0, 64), P("ua", 64, 128), OP.mult, 64, two=True)
        v_ts(P("uk", 0, 64), P("up", 0, 64), 5, 8191, OP.arith_shift_right, OP.bitwise_and, 64)
        v_tt(PD("us"), P("uk", 0, 64), P("psU", 128, 192), OP.add, 64)
        v_ts(PD("uq"), PD("us"), MAGIC, -MAGIC, OP.add, OP.add, 64)
        rt = lambda k, i: (n("rt" + x), 144 * k, i)
        nxt = [[rt(1, "ib"), (n("x0"), 0, "ib")], [rt(2, "ib"), (n("x1"), 0, "ib"), (n("x2"), 0, "ib")]]
        hp = A(Ep, 0, NJ)
        hm = [x_[:4] + (False,) for x_ in LL(Ep, 0, [(n("us"), 0, "ifp"), (n("uq"), 0, "inb")])]
        pe(hm + [(hp, A("i32b", 0, 128), A(mf, 0, NJ), False, True)], 512 + 128 + 64)
        v_ts(A(n("off"), 0, NJ), hp, 4095.5, None, OP.add, None, NJ)
        s_act(A(n("cod"), 0, NJ), hp, NJ, bias=float(32 * 4095.5 + (s + 1) * 2 ** 18), scale=32.0)
        nq = (3, 2, 1)[s]
        if s < 2:
            mm = LL(Ep, 2 * NJ, nxt[s])
            pe([x_[:4] + (False,) for x_ in mm[:-2]], 64 * len(mm) - 128)
        c1 = CH - DS
        k1 = c1 // 16
        sv, pd = A(n("sv"), 0, DS), A(U, 256, 256 + DS)
        s_act(sv, IND("mks", 0, WT, n("off"), k1, NJ), DS, ind=True)
        v_tt(A(n("d"), 0, c1), IND("mks", 0, WT, n("off"), 0, k1), A(qb, b, b + c1), OP.subtract, c1, ind=True)
        pe([(pd, A("ib", 0, 128), sv, True, False), (pd, A("inb", 0, 128), A(qb, b + c1, b + CH), False, True)], 2 * DS)
        s_act(A(n("d"), c1, CH), pd, DS)
        pe(TL(D, n("d"), 0, A("rd", 0, 8 * nq), nq), 16 * 48)
        s_act(P("an", 0, 64), P("psD", 0, 64), 64, func=AF.Abs)
        if s < 2:
            w = 64 * nq - 64
            v_tt(P("psU", 0, w), P("psD", 64, 64 + w), P("zc" + x, 0, 128) if s == 0 else P("e1", 0, 64), OP.add, w)
        v_tt(PD("hit"), P("an", 0, 64), P("psU", 192, 256), OP.is_lt, 64)
        pe(LL(D, 448, [(n("hit"), 0, "ib")]), 128)
        if s < 2:
            v_tt(PD("x0" if s == 0 else "x2"), PD("hit"), P("psU", 0, 64), OP.mult, 64)
            if s == 0:
                v_tt(PD("x1"), PD("hit"), P("psU", 64, 128), OP.mult, 64)
                v_tt(P("e1", 0, 64), P("zc" + x, 128, 192), PD("x1"), OP.subtract, 64, two=True)
            pe(mm[-2:], 128)
        yb_ = A(n("bb") if s == 0 else n("y"), 0, NJ)
        v_tt(yb_, A(D, 448, 448 + NJ), A(n("cod"), 0, NJ), OP.mult, NJ)
        if c == 0 and r < 2:
            v_ts(A("emg", 0, 8), A(mo, 0, 8), 0.0, None, OP.is_gt, None, 8)
            v_tt(A("ecf", 0, 8), A("emg", 0, 8), A(n("cod"), 0, 8), OP.mult, 8)
            v_tt(A("eyf" if s else "ef", 0, 8), A("ecf", 0, 8), A(yb_[1][0][0], 0, 8), OP.subtract, 8)
            if s:
                v_tt(A("ef", 0, 8), A("ef", 0, 8), A("eyf", 0, 8), OP.max, 8)
        if s < 2:
            v_cp(A(n("mo"), 0, NJ), A(Ep, 2 * NJ, 3 * NJ), NJ)
            s_act(A(n("ms"), 0, NJ), A(Ep, 2 * NJ, 3 * NJ), NJ)
        if s:
            v_tt(A(n("bb"), 0, NJ), A(n("bb"), 0, NJ), A(n("y"), 0, NJ), OP.max, NJ, two=True)

    def learn(r, c, sends):
        n = lambda b: "%s_%d" % (b, c)
        v_cp(A(n("bi"), 0, NJ), A(n("bb"), 0, NJ), NJ)
        v_ts(A(n("bm"), 0, NJ), A(n("bi"), 0, NJ), 31, None, OP.bitwise_and, None, NJ)
        v_ts(A(n("bc"), 0, NJ), A(n("bi"), 0, NJ), 5, 8191, OP.arith_shift_right, OP.bitwise_and, NJ)
        v_cp(A(n("ofb"), 0, NJ), A(n("bc"), 0, NJ), NJ)
        v_cp(A(n("ofm"), 0, NJ), A(n("bm"), 0, NJ), NJ)
        for h in range(2):
            s = 2 * c + h
            q = A("q%d" % r, NB * s, NB * s + NB)
            dl, zl = A(n("dl"), NB * h, NB * h + NB), A(n("zl"), NB * h, NB * h + NB)
            ps = A("psL%d" % h, 0, NB)
            v_tt(dl, IND("mks", 0, WT, n("ofb"), 24 * h, 24 * h + 24), q, OP.subtract, NB, ind=True)
            v_tt(zl, IND("ml", 0, 16, n("ofm"), 24 * h, 24 * h + 24), dl, OP.mult, NB, ind=True)
            pe([(ps, A("ib", 0, 128), q, True, False), (ps, A("ib", 0, 128), zl, False, True)], 2 * NB)
            if r < 2 and s == rank:
                s_act(A("q%d" % (r + 1), NB * s, NB * s + NB), ps, NB)
            else:
                o = A("n%d" % r, NB * s, NB * s + NB)
                s_act(o, ps, NB)
                if r < 2:
                    sends.append(send(T.cores[s], T["q%d" % (r + 1)][:, NB * rank:NB * rank + NB], o, "a%d_%d" % (r + 1, rank)))
                else:
                    dma("Q", ext(T.yq[:, NB * s:NB * s + NB]), o, 3.0)
        if r == 2:
            v_ts(A(n("nb"), 0, NJ), A(n("bm"), 0, NJ), 0, None, OP.is_equal, None, NJ)
            o = A("yb_s", NJ * c, NJ * c + NJ)
            v_tt(o, A(n("bc"), 0, NJ), A(n("nb"), 0, NJ), OP.subtract, NJ, two=True)
            dma("Q", ext(T.yb[:, NJ * c:NJ * c + NJ]), o, 3.0)

    def edits_choose(r):
        e8, e16 = (lambda b: A(b, 0, 8)), (lambda b: A(b, 0, 16))
        v_tt(e8("eg"), e8("ef"), e8("bb_0"), OP.is_gt, 8)
        v_tt(e8("eed"), e8("eg"), e8("bb_0"), OP.min, 8)
        v_cp(e8("efi"), e8("ef"), 8)
        v_ts(e8("efc"), e8("efi"), 5, 8191, OP.arith_shift_right, OP.bitwise_and, 8)
        v_ts(e8("emf"), e8("efi"), 31, None, OP.bitwise_and, None, 8)
        v_ts(e8("ekk"), e8("bi_0"), 18, None, OP.arith_shift_right, None, 8)
        v_tt(A("eu", 0, 8), e8("efc"), A("tr", 0, 8), OP.subtract, 8)
        v_tt(A("eu", 8, 16), e8("bc_0"), A("tr", 0, 8), OP.subtract, 8)
        v_tt(A("ev", 0, 8), A("eu", 0, 8), e8("eed"), OP.mult, 8)
        v_tt(A("ev", 8, 16), A("eu", 8, 16), e8("eed"), OP.mult, 8)
        v_tt(e16("efb"), e16("ev"), e16("tr"), OP.add, 16)
        v_cp(e16("eof"), e16("efb"), 16)
        v_cp(e8("eok"), e8("ekk"), 8)
        v_cp(e8("eom"), e8("emf"), 8)
        v_tt(A("eka", 0, 256), IND("kt", 0, WT, "eof", 0, 16), A("tidx", 0, 256), OP.add, 256, ind=True)
        v_ts(e16("en1"), e16("efb"), -128.0, None, OP.mult, None, 16)
        v_tt(e16("enb"), e16("en1"), e16("half"), OP.subtract, 16)
        v_tt(e16("eg2"), e16("tr"), e16("efb"), OP.subtract, 16)
        for k in range(16):
            w = 16 * (k % 8 + 1)
            f = 128 * (k // 8)
            s_act(A("ey", 128 * k, 128 * k + w), A("eka", f, f + w), w, bias=A("enb", k, k + 1))
            o, i = A("emn", k, k + 1), A("ey", 128 * k, 128 * k + w)
            add("V", lambda inc, o=o, i=i: inc(g.vector.tensor_reduce(o[0], i[0], AxisListType.X, OP.min, apply_absolute_value=True)),
                [o], [i], vc(w))
        v_tt(e16("els"), e16("emn"), e16("half"), OP.is_le, 16)
        v_tt(e16("eg3"), e16("eg2"), e16("els"), OP.mult, 16)
        v_tt(e16("efn"), e16("efb"), e16("eg3"), OP.add, 16)
        v_cp(e16("eow"), e16("efn"), 16)
        s_act(A("evv", 0, 128), IND("mks", 0, WT, "ofb_0", 0, 8), 128, ind=True, func=AF.Copy)
        v_tt(A("ev1", 0, 128), IND("k1", 0, 16, "eok", 0, 8), A("evv", 0, 128), OP.mult, 128, ind=True)
        s_act(A("ezz", 0, 128), IND("mt", 0, 16, "eom", 0, 8), 128, ind=True, func=AF.Copy)

    def edits_write(r):
        m = lambda b: A(b, 0, 128)
        ps = m("psL0")
        pe([(ps, m("sym"), A("q%d" % r, 0, 128), True, False), (ps, m("sh12"), m("ev1"), False, False),
            (ps, m("sh2"), m("evv"), False, True)], 3 * 128)
        s_act(m("eww"), ps, 128)
        v_cp(IND("mks", 0, WT, "eow", 0, 8), m("eww"), 128, cost=0.05 + 128 * 3.5 * CY)
        s_act(m("emm"), IND("mks", 0, WT, "eow", 8, 16), 128, ind=True, func=AF.Copy)
        ps = m("psL1")
        pe([(ps, m("sel"), m("ezz"), True, False), (ps, m("sd"), m("emm"), False, True)], 2 * 128)
        s_act(m("enn"), ps, 128)
        v_cp(IND("mks", 0, WT, "eow", 8, 16), m("enn"), 128, cost=0.05 + 128 * 3.5 * CY)

    for r in range(3):
        for s in range(3):
            for c in CO:
                step(r, s, c)
            if r == 0 and s == 1:
                late_constants()
            if r == 0 and s == 2:
                ropes_b()
        for c in CO:
            sends = []
            learn(r, c, sends)
            if c == 0 and r < 2:
                edits_choose(r)
            if r < 2:
                for s in others:
                    if s // 2 == c:
                        arrive(A("q%d" % (r + 1), NB * s, NB * s + NB), s, "a%d_%d" % (r + 1, s), sends, 5.0)
        if r < 2:
            edits_write(r)

    nop = len(ops)
    succ = [[] for _ in range(nop)]
    for o in ops:
        for d in o["dep"]:
            succ[d].append(o["i"])
    prio = [0.0] * nop
    for i in range(nop - 1, -1, -1):
        o = ops[i]
        prio[i] = o["cost"] + o["lat"] + LAT + max([prio[k] for k in succ[i]] + [0.0])
    left = [len(o["dep"]) for o in ops]
    ready = {"V": [], "S": [], "P": [], "G": [], "Q": [], "X": []}
    at = [0.0] * nop
    free = {e: 0.0 for e in ready}
    for o in ops:
        if not left[o["i"]]:
            ready[o["eng"]].append(o["i"])
    order = []
    while len(order) < nop:
        best = None
        for e in ready:
            for i in ready[e]:
                st = max(at[i], free[e])
                k = (st, -prio[i], i)
                if best is None or k < best[0]:
                    best = (k, i, e, st)
        _k, i, e, st = best
        ready[e].remove(i)
        o = ops[i]
        end = st + o["cost"]
        if e != "X":
            free[e] = end
        order.append(i)
        for k in succ[i]:
            at[k] = max(at[k], end + o["lat"] + LAT)
            left[k] -= 1
            if not left[k]:
                ready[ops[k]["eng"]].append(k)

    queue = {"V": g.vector, "S": g.scalar, "P": g.tensor, "G": g, "Q": g.sync}
    count = {e: 0 for e in queue}
    known = {e: {} for e in queue}
    done = [None] * nop
    for i in order:
        o = ops[i]
        e = o["eng"]
        if e == "X":
            done[i] = (o["sem"], o["val"], {})
            continue
        kn = known[e]
        need = {}
        src = {}
        for d, kind in sorted(o["dep"].items(), key=lambda kv: -kv[0]):
            sem, val, vcl = done[d]
            if sem == "" or kind == 0 or (e == "P" and ops[d]["eng"] == "P"):
                continue
            if kn.get(sem, 0) >= val:
                continue
            need[sem] = max(need.get(sem, 0), val)
            src[(sem, val)] = vcl
        for sem in list(need):
            for (s2, v2), vcl in src.items():
                if s2 != sem and s2 in need and need[s2] >= v2 and vcl.get(sem, 0) >= need[sem]:
                    del need[sem]
                    break
        for sem in need:
            queue[e].wait_ge(T.sem[sem], need[sem])
        for (s2, v2), vcl in src.items():
            for k, v in list(vcl.items()) + [(s2, v2)]:
                if kn.get(k, 0) < v:
                    kn[k] = v
        if o["sem"] is None:
            own = "s" + e
            o["fn"](lambda ins: ins.then_inc(T.sem[own], 1))
            count[e] += o["cnt"]
            done[i] = (own, count[e], dict(kn))
        else:
            o["fn"](None)
            done[i] = (o["sem"], o["val"], dict(kn))

    for e in ("V", "S", "P", "G"):
        g.wait_ge(T.sem["s" + e], count[e])
    for k in range(ndma[0]):
        g.wait_ge(T.sem["d%d" % k], 16)
    for s, v in arrivals:
        g.wait_ge(T.sem[s], v)
    g.wait_ge(T.sem["loc"], nsend[0])
